import numpy as np
import ml_dtypes


def mxq(x, axis, fmt="e4m3"):
    dtype, down = {"e4m3": (ml_dtypes.float8_e4m3fn, 7), "e5m2": (ml_dtypes.float8_e5m2, 14)}[fmt]
    v = np.moveaxis(np.asarray(x, np.float32).astype(ml_dtypes.bfloat16).astype(np.float64), axis, -1)
    blocks = v.reshape(v.shape[:-1] + (-1, 32))
    amax = np.abs(blocks).max(-1, keepdims=True)
    byte = np.maximum(np.where(amax > 0, np.frexp(amax)[1] - 1 + 127, 0) - down, 1)
    scale = np.exp2(byte - 127.0)
    codes = (blocks / scale).astype(np.float32).astype(dtype).astype(np.float64)
    return np.moveaxis((codes * scale).reshape(v.shape), -1, axis)


WIDE = False


def mx_kscale(k):
    if not WIDE:
        return np.ones(k)
    levels = np.array([10, -10, 5, -5, 0])
    if k % 512:
        return np.exp2(np.random.permutation(np.resize(levels, k // 32))).repeat(32)
    a = np.empty((k // 512, 16))
    for p in range(k // 512):
        a[p, :8] = np.random.permutation(np.resize(levels, 8))
        for g in range(8):
            far = levels[np.abs(levels - a[p, g]) >= 10]
            a[p, g + 8] = far[np.random.randint(len(far))]
    return np.exp2(a.ravel()).repeat(32)


def f64(x):
    return np.asarray(x).astype(np.float64)


def striped(idx):
    return np.tile(np.asarray(idx).reshape(-1, 16).T, (8, 1)).astype(np.uint16)


def unstriped(offs):
    return offs[:16].T.reshape(-1).astype(np.int64)


E2M1 = np.array([0.0, 0.5, 1.0, 1.5, 2.0, 3.0, 4.0, 6.0, -0.0, -0.5, -1.0, -1.5, -2.0, -3.0, -4.0, -6.0])


def pack_weight(w, fmt):
    k, n = w.shape
    w = f64(np.asarray(w, np.float32).astype(ml_dtypes.bfloat16)).reshape(k // 32, 32, n)
    amax = np.abs(w).max(1)
    if fmt == "e4m3":
        byte = np.frexp(amax)[1] - 1 + 127 - 7
    else:
        mant, ex = np.frexp(amax / 6.0)
        byte = np.where(mant > 0.5, ex, ex - 1) + 127
    byte = np.clip(np.where(amax > 0, byte, 1), 1, 254)
    scaled = (w * np.exp2(127.0 - byte)[:, None, :]).reshape(k, n).astype(np.float32)
    by_word = np.ascontiguousarray(scaled.reshape(k // 512, 128, 4, n).transpose(0, 1, 3, 2))
    if fmt == "e4m3":
        words = by_word.astype(ml_dtypes.float8_e4m3fn).view(np.uint8)
    else:
        c = by_word.astype(ml_dtypes.float4_e2m1fn).view(np.uint8) & 0xF
        words = (c[..., 0::2] | (c[..., 1::2] << 4)).reshape(k // 512, 128, 2 * n)
    return np.ascontiguousarray(words), np.ascontiguousarray(byte.astype(np.uint8).reshape(k // 512, 16, n))


def unpack_weight(words, scales, fmt):
    g, _, n = scales.shape
    words = np.ascontiguousarray(words).reshape(g, 128, n, -1)
    if fmt == "e4m3":
        vals = words.view(ml_dtypes.float8_e4m3fn).astype(np.float64)
    else:
        nib = np.empty((g, 128, n, 4), np.uint8)
        nib[..., 0::2] = words & 0xF
        nib[..., 1::2] = words >> 4
        vals = E2M1[nib]
    vals = vals * np.repeat(np.exp2(scales.astype(np.float64) - 127.0), 8, axis=1)[..., None]
    return vals.transpose(0, 1, 3, 2).reshape(g * 512, n)


def bf(x):
    return np.asarray(x, np.float32).astype(ml_dtypes.bfloat16)


def planes(Y):
    r, m = Y.shape
    b = f64(bf(Y)).reshape(r // 32, 32, m)
    amax = np.abs(b).max(1)
    byte = np.clip(np.where(amax > 0, np.frexp(amax)[1] - 1 + 127 - 7, 1), 1, 254)
    codes = (b * np.exp2(127.0 - byte)[:, None, :]).reshape(r, m).astype(np.float32).astype(ml_dtypes.float8_e4m3fn).view(np.uint8)
    words = codes.reshape(r // 512, 128, 4, m).transpose(0, 1, 3, 2)
    return np.ascontiguousarray(words), np.ascontiguousarray(byte.astype(np.uint8).reshape(r // 512, 16, m))


D, T, G, I, Q, E = 512, 2048, 256, 512, 256, 512


def setup_inputs():
    n = np.random.standard_normal
    idx = np.random.permutation(T)[:G]
    idx2 = np.random.randint(0, G, I)
    idx3 = np.random.randint(0, G, I)
    idx4 = np.random.permutation(T)[:I]
    fd = mx_kscale(D)
    fi = mx_kscale(I)
    ti = np.ones(T)
    ti[idx4] = fi
    keysp = pack_weight(n((D, T)) / fd[:, None], "e2m1")
    return {
        "query": (n((D, Q)) * 0.6 / np.sqrt(D) * fd[:, None]).astype(np.float32),
        "keys_words": keysp[0],
        "keys_scales": keysp[1],
        "near": (np.random.uniform(0.05, 0.95, (1, I))).astype(np.float32),
        "bias": (np.random.uniform(-0.5, 0.5, (1, I))).astype(np.float32),
        "size": (np.random.uniform(0.5, 2.0, (1, I)) * fi).astype(np.float32),
        "vals": (n((E, T)) / ti).astype(np.float32),
        "offs": striped(idx),
        "offs2": striped(idx2),
        "offs3": striped(idx3),
        "offs4": striped(idx4),
    }


def reference(query, keys_words, keys_scales, near, bias, size, vals, offs, offs2, offs3, offs4):
    idx = unstriped(offs)
    idx2 = unstriped(offs2)
    idx3 = unstriped(offs3)
    idx4 = unstriped(offs4)
    keysu = unpack_weight(keys_words, keys_scales, "e2m1")
    queryq = mxq(f64(query), 0, "e4m3")
    keysidxg = keysu[:, idx]
    a = queryq.T @ keysidxg
    s = a[:, idx2] * f64(near) + a[:, idx3] * (1.0 - f64(near)) + f64(bias)
    p = np.exp(s - np.max(s, axis=1, keepdims=True))
    w = p * f64(size) / np.sum(p, axis=1, keepdims=True)
    wt = w.T
    vt = f64(vals)[:, idx4].T
    vtq = mxq(vt, 0, "e4m3")
    wtq = mxq(wt, 0, "e4m3")
    o = vtq.T @ wtq
    words, scales = planes(o)
    return o, words, scales

@@ -1,0 +1,240 @@
+from contextlib import ExitStack
+
+import concourse.mybir as mybir
+from concourse.masks import make_identity
+
+D, T, G, I, Q, E = 512, 2048, 256, 512, 256, 512
+FLOPS = 2 * D * Q * G + 2 * I * E * Q
+
+F32 = mybir.dt.float32
+BF16 = mybir.dt.bfloat16
+I32 = mybir.dt.int32
+U32 = mybir.dt.uint32
+U16 = mybir.dt.uint16
+U8 = mybir.dt.uint8
+FP8X4 = mybir.dt.float8_e4m3fn_x4
+FP4X4 = mybir.dt.float4_e2m1fn_x4
+ALU = mybir.AluOpType
+ACT = mybir.ActivationFunctionType
+AX = mybir.AxisListType
+
+P = 128
+PACK = 4
+Q_TILES = Q // P
+WINDOW = 544
+
+
+def tile_attend_betweenanchors_pl_kernel(tc, query, keys_words, keys_scales, near, bias, size, vals,
+                                          offs, offs2, offs3, offs4, out_0, out_1, out_2):
+    nc = tc.nc
+    with ExitStack() as ctx:
+        sb = ctx.enter_context(tc.tile_pool(name="sb", bufs=1))
+        reused = ctx.enter_context(tc.tile_pool(name="reused", bufs=1))
+        ps = ctx.enter_context(tc.psum_pool(name="ps", bufs=1))
+        places = {
+            "bias_cols": 0, "rounded": 0,
+            "query0_codes": 28672, "query_grouped1": 28672, "from_right0": 28672,
+            "turned0": 4096, "picked1": 4096,
+            "p0": 6144, "picked2": 6144, "picked3": 6144,
+            "turned1": 8192, "neg_max0": 10240 - 64, "picked0": 10240,
+            "val_pool2": 12288, "neg_max1": 12288,
+            "val_pool3": 20480, "w1": 20480, "inverse1": 21504, "w0_codes": 22528, "v0_codes": 23040,
+            "v1_codes": 23552, "v2_codes": 24064,
+        }
+
+        def sbuf(name, shape, dtype):
+            if name in places:
+                return reused.tile(shape, dtype, name=name, align_bytes=64, offset=places[name])
+            return sb.tile(shape, dtype, name=name, align_bytes=64)
+
+        def bank(number, name, shape):
+            return ps.tile(shape, F32, name=name, tag="bank%d" % number)
+
+        def load_list(name, src):
+            tile = sb.tile(list(src.shape), U16, name=name)
+            nc.sync.dma_start(tile[:], src)
+            return tile
+
+        def load_columns(name, row, queue):
+            tile = sbuf(name, [P, PACK], F32)
+            queue.dma_start(tile[:], row.rearrange("o (p t) -> (o p) t", t=PACK))
+            return tile
+
+        key_scale_pool = sbuf("key_scale_pool", [P, T], U8)
+        nc.gpsimd.memset(key_scale_pool[:].bitcast(I32), 0)
+        anchors = load_list("anchors", offs)
+        near_cols = load_columns("near_cols", near, nc.sync)
+        query_rows = query.rearrange("(p j) q -> p j q", j=PACK)
+        query_raw = [sbuf("query_raw%d" % h, [P, PACK, P], F32) for h in range(Q_TILES)]
+        nc.sync.dma_start(query_raw[0][:], query_rows[:, :, :P])
+        for quad in range(4):
+            nc.sync.dma_start(key_scale_pool[32 * quad:32 * quad + 4, :].bitcast(I32),
+                                keys_scales[0, 4 * quad:4 * quad + 4, :].bitcast(I32))
+        key_word_pool = sbuf("key_word_pool", [P, T], U16)
+        nc.sync.dma_start(key_word_pool[:].bitcast(I32), keys_words[0].bitcast(I32))
+        left = load_list("left", offs2)
+        nc.sync.dma_start(query_raw[1][:], query_rows[:, :, P:])
+        right = load_list("right", offs3)
+        vals_by_place = vals.rearrange("(p r) t -> p r t", r=PACK)
+        val_pool = []
+        for r in range(PACK):
+            tile = sbuf("val_pool%d" % r, [P, T], F32)
+            nc.sync.dma_start(tile[:], vals_by_place[:, r, :])
+            val_pool.append(tile)
+            if r == 0:
+                bias_cols = load_columns("bias_cols", bias, nc.sync)
+                tokens = load_list("tokens", offs4)
+            if r == 1:
+                size_cols = load_columns("size_cols", size, nc.sync)
+
+        ident = sbuf("ident", [P, P], F32)
+        make_identity(nc, ident[:])
+        windows = []
+        for h in range(Q_TILES):
+            tile = sbuf("scores%d" % h, [P, WINDOW], F32)
+            nc.gpsimd.memset(tile[:, G:], 0.0)
+            windows.append(tile)
+
+        def spread(number, name, cols):
+            tile = bank(number, name, [P, PACK, P])
+            for t in range(PACK):
+                nc.tensor.transpose(tile[:, t, :], cols[:, t:t + 1].to_broadcast([P, P]), ident[:])
+            return tile[:].rearrange("q t p -> q p t")
+
+        def by_place(tile):
+            return tile[:].rearrange("q (p t) -> q p t", t=PACK)
+
+        near_ps = spread(0, "near_ps", near_cols)
+        near_row = sbuf("near_row", [P, I], F32)
+        far_row = sbuf("far_row", [P, I], F32)
+        nc.scalar.activation(by_place(near_row), near_ps, ACT.Copy)
+        nc.scalar.activation(by_place(far_row), near_ps, ACT.Copy, bias=1.0, scale=-1.0)
+
+        key_scales = sbuf("key_scales", [P, G], U8)
+        nc.vector.tensor_copy(key_scales[:], key_scale_pool[:].indirect(anchors[:]))
+        key_words = sbuf("key_words", [P, G], U16)
+
+        def quantise(name, grouped):
+            codes = sbuf(name + "_codes", [P, P], U32)
+            scales = sbuf(name + "_scales", [P, P], U8)
+            nc.vector.quantize_mx(out=codes[:].bitcast(FP8X4), scales=scales[:], in_=grouped[:])
+            return codes, scales
+
+        for h in range(Q_TILES):
+            grouped = sbuf("query_grouped%d" % h, [P, P * PACK], BF16)
+            (nc.vector.tensor_copy if h == 0 else nc.scalar.copy)(
+                grouped[:].rearrange("p (c i t) -> p c t i", i=4, t=PACK),
+                query_raw[h][:].rearrange("p t (c i) -> p c t i", i=4))
+            codes, scales = quantise("query%d" % h, grouped)
+            if h == 0:
+                nc.vector.tensor_copy(key_words[:], key_word_pool[:].indirect(anchors[:]))
+            acc = bank(3 * h, "scores_ps%d" % h, [P, G])
+            nc.tensor.matmul_mx(out=acc[:], lhsT=codes[:].bitcast(FP8X4), lhsT_scale=scales[:],
+                                rhs=key_words[:].bitcast(FP4X4), rhs_scale=key_scales[:], start=True, stop=True)
+            nc.scalar.copy(windows[h][:, :G], acc[:])
+
+        bias_ps = spread(0, "bias_ps", bias_cols)
+        bias_row = sbuf("bias_row", [P, I], F32)
+        nc.scalar.copy(by_place(bias_row), bias_ps)
+        size_ps = spread(3, "size_ps", size_cols)
+
+        def turn_and_add(acc, terms):
+            for n, term in enumerate(terms):
+                for c in range(PACK):
+                    nc.tensor.matmul(acc[:, c * P:(c + 1) * P], lhsT=term[:, c * P:(c + 1) * P], rhs=ident[:],
+                                     is_transpose=True, start=(n == 0 and c == 0),
+                                     stop=(n == len(terms) - 1 and c == PACK - 1))
+
+        slot_scores = []
+        def look_up(h):
+            from_left = sbuf("from_left%d" % h, [P, I], F32)
+            nc.vector.tensor_tensor(from_left[:], windows[h][:].indirect(left[:]), near_row[:], ALU.mult)
+            from_right = sbuf("from_right%d" % h, [P, I], F32)
+            nc.vector.tensor_tensor(from_right[:], windows[h][:].indirect(right[:]), far_row[:], ALU.mult)
+            return from_left, from_right
+
+        def add_up(h, from_left, from_right):
+            turned_ps = bank(4, "turned_ps%d" % h, [P, I])
+            turn_and_add(turned_ps, [bias_row, from_left, from_right])
+            turned = sbuf("turned%d" % h, [P, I], F32)
+            nc.scalar.copy(turned[:], turned_ps[:])
+            back = bank(6 + h, "slot_scores%d" % h, [P, I])
+            for c in range(PACK):
+                nc.tensor.transpose(back[:, c * P:(c + 1) * P], turned[:, c * P:(c + 1) * P], ident[:])
+            slot_scores.append(back)
+
+        def turn_words(number, name, rows):
+            words = rows[:].bitcast(F32)
+            acc = bank(number, name + "_ps", [P, 2, P])
+            for u in range(2):
+                nc.tensor.transpose(acc[:, u, :], words[:, u::2], ident[:])
+            grouped = sbuf(name + "_grouped", [P, P * PACK], BF16)
+            nc.scalar.copy(grouped[:].bitcast(F32).rearrange("p (c u) -> p c u", u=2),
+                           acc[:].rearrange("p u c -> p c u"))
+            return grouped
+
+        def softmax_head(h):
+            neg_max = sbuf("neg_max%d" % h, [P, 32], F32)[:, 0:1]
+            nc.vector.tensor_reduce(neg_max, slot_scores[h][:], AX.X, ALU.max, negate=True)
+            p = sbuf("p%d" % h, [P, I], F32)
+            total = sbuf("total%d" % h, [P, 1], F32)
+            nc.scalar.activation(p[:], slot_scores[h][:], ACT.Exp, bias=neg_max, accum_out=total[:])
+            return p, total
+
+        def softmax_tail(h, p, total):
+            inverse = sbuf("inverse%d" % h, [P, 1], F32)
+            nc.vector.reciprocal(inverse[:], total[:])
+            w = sbuf("w%d" % h, [P, I], BF16)
+            nc.vector.scalar_tensor_tensor(by_place(w), by_place(p), inverse[:], size_ps, ALU.mult, ALU.mult)
+            return turn_words(2, "w%d" % h, w)
+
+        def gather_values(r):
+            picked = sbuf("picked%d" % r, [P, I], BF16)
+            if r == 0:
+                rounded = sbuf("rounded", [P, T], BF16)
+                for c in range(0, T, 512):
+                    nc.scalar.activation(rounded[:, c:c + 512], val_pool[r][:, c:c + 512], ACT.Copy)
+                nc.scalar.activation(picked[:], rounded[:].indirect(tokens[:]), ACT.Copy)
+            else:
+                nc.vector.tensor_copy(picked[:], val_pool[r][:].indirect(tokens[:]))
+            return turn_words((0, 1, 0, 1)[(1, 0, 2, 3).index(r)], "v%d" % r, picked)
+
+        out_scales = sbuf("out_scales", [P, Q], U8)
+        out_rows = out_0.rearrange("(p r) q -> p r q", r=PACK)
+        out_words = out_1[0].rearrange("p q r -> p (q r)").bitcast(I32)
+
+        def finish(h, w_mx, v_mx):
+            cols = slice(h * P, (h + 1) * P)
+            acc = bank(5 - h, "out_ps%d" % h, [P, PACK, P])
+            for r in range(PACK):
+                nc.tensor.matmul_mx(out=acc[:, r, :], lhsT=v_mx[r][0][:].bitcast(FP8X4), lhsT_scale=v_mx[r][1][:],
+                                    rhs=w_mx[0][:].bitcast(FP8X4), rhs_scale=w_mx[1][:], start=True, stop=True)
+            grouped = sbuf("out_grouped%d" % h, [P, P * PACK], BF16)
+            (nc.scalar.copy if h == 0 else nc.vector.tensor_copy)(
+                grouped[:].rearrange("p (q r) -> p q r", r=PACK), acc[:].rearrange("p r q -> p q r"))
+            result = sbuf("result%d" % h, [P, PACK, P], F32)
+            nc.scalar.copy(result[:], acc[:])
+            nc.scalar.dma_start(out_rows[:, :, cols], result[:])
+            codes = sbuf("out_codes%d" % h, [P, P], I32)
+            nc.vector.quantize_mx(out=codes[:].bitcast(FP8X4), scales=out_scales[:, cols], in_=grouped[:])
+            nc.sync.dma_start(out_words[:, cols], codes[:])
+
+        looked_up = [look_up(h) for h in range(Q_TILES)]
+        add_up(0, *looked_up[0])
+        p0 = softmax_head(0)
+        add_up(1, *looked_up[1])
+        v_grouped = {1: gather_values(1)}
+        w0 = softmax_tail(0, *p0)
+        v_grouped[0] = gather_values(0)
+        v_grouped[2] = gather_values(2)
+        p1 = softmax_head(1)
+        v_grouped[3] = gather_values(3)
+        w1 = softmax_tail(1, *p1)
+        w0_mx = quantise("w0", w0)
+        v_mx = [quantise("v%d" % r, v_grouped[r]) for r in range(PACK)]
+        finish(0, w0_mx, v_mx)
+        finish(1, quantise("w1", w1), v_mx)
+        for quad in range(4):
+            queue = nc.sync if quad % 2 == 0 else nc.scalar
+            queue.dma_start(out_2[0, 4 * quad:4 * quad + 4, :].bitcast(I32),
+                            out_scales[32 * quad:32 * quad + 4, :].bitcast(I32))

@@ -21,7 +21,8 @@ AX = mybir.AxisListType
 P = 128
 PACK = 4
 Q_TILES = Q // P
-WINDOW = 544
+WINDOW = 704
+CHUNKS = I // P
 
 
 def tile_attend_betweenanchors_pl_kernel(tc, query, keys_words, keys_scales, near, bias, size, vals,
@@ -29,22 +30,23 @@ def tile_attend_betweenanchors_pl_kernel(tc, query, keys_words, keys_scales, nea
     nc = tc.nc
     with ExitStack() as ctx:
         sb = ctx.enter_context(tc.tile_pool(name="sb", bufs=1))
-        reused = ctx.enter_context(tc.tile_pool(name="reused", bufs=1))
+        shared = ctx.enter_context(tc.tile_pool(name="shared", bufs=1))
         ps = ctx.enter_context(tc.psum_pool(name="ps", bufs=1))
-        places = {
-            "bias_cols": 0, "rounded": 0,
-            "query0_codes": 28672, "query_grouped1": 28672, "from_right0": 28672,
-            "turned0": 4096, "picked1": 4096,
-            "p0": 6144, "picked2": 6144, "picked3": 6144,
-            "turned1": 8192, "neg_max0": 10240 - 64, "picked0": 10240,
-            "val_pool2": 12288, "neg_max1": 12288,
-            "val_pool3": 20480, "w1": 20480, "inverse1": 21504, "w0_codes": 22528, "v0_codes": 23040,
-            "v1_codes": 23552, "v2_codes": 24064,
-        }
+
+        pool_bytes = 4 * T
+        places = {"val_pool%d" % r: r * pool_bytes for r in range(PACK)}
+        for h in range(Q_TILES):
+            places["query_raw%d" % h] = (2 * h + 1) * pool_bytes - 1024
+        tenants = (["neg_max0"], ["neg_max1", "inverse0", "v0_codes"], [], ["v1_codes", "w0_codes", "w1_codes", "v2_codes"])
+        places["key_scale_pool"] = places["query0_codes"] = PACK * pool_bytes
+        places["query_grouped1"] = places["from_left0"] = PACK * pool_bytes + T
+        for r in range(PACK):
+            for n, name in enumerate(tenants[r]):
+                places[name] = r * pool_bytes + 2048 + 512 * n
 
         def sbuf(name, shape, dtype):
             if name in places:
-                return reused.tile(shape, dtype, name=name, align_bytes=64, offset=places[name])
+                return shared.tile(shape, dtype, name=name, align_bytes=64, offset=places[name])
             return sb.tile(shape, dtype, name=name, align_bytes=64)
 
         def bank(number, name, shape):
@@ -55,26 +57,30 @@ def tile_attend_betweenanchors_pl_kernel(tc, query, keys_words, keys_scales, nea
             nc.sync.dma_start(tile[:], src)
             return tile
 
-        def load_columns(name, row, queue):
-            tile = sbuf(name, [P, PACK], F32)
-            queue.dma_start(tile[:], row.rearrange("o (p t) -> (o p) t", t=PACK))
-            return tile
-
         key_scale_pool = sbuf("key_scale_pool", [P, T], U8)
         nc.gpsimd.memset(key_scale_pool[:].bitcast(I32), 0)
+        slot_rows = sbuf("slot_rows", [P, P], F32)
+        nc.gpsimd.memset(slot_rows[:], 0.0)
+
+        def load_rows(place, row):
+            nc.sync.dma_start(slot_rows[32 * place:32 * place + CHUNKS, :],
+                              row.rearrange("o (c p) -> (o c) p", p=P))
+
         anchors = load_list("anchors", offs)
-        near_cols = load_columns("near_cols", near, nc.sync)
         query_rows = query.rearrange("(p j) q -> p j q", j=PACK)
         query_raw = [sbuf("query_raw%d" % h, [P, PACK, P], F32) for h in range(Q_TILES)]
         nc.sync.dma_start(query_raw[0][:], query_rows[:, :, :P])
         for quad in range(4):
             nc.sync.dma_start(key_scale_pool[32 * quad:32 * quad + 4, :].bitcast(I32),
-                                keys_scales[0, 4 * quad:4 * quad + 4, :].bitcast(I32))
+                              keys_scales[0, 4 * quad:4 * quad + 4, :].bitcast(I32))
         key_word_pool = sbuf("key_word_pool", [P, T], U16)
         nc.sync.dma_start(key_word_pool[:].bitcast(I32), keys_words[0].bitcast(I32))
         left = load_list("left", offs2)
         nc.sync.dma_start(query_raw[1][:], query_rows[:, :, P:])
         right = load_list("right", offs3)
+        load_rows(0, near)
+        load_rows(1, bias)
+        load_rows(2, size)
         vals_by_place = vals.rearrange("(p r) t -> p r t", r=PACK)
         val_pool = []
         for r in range(PACK):
@@ -82,10 +88,7 @@ def tile_attend_betweenanchors_pl_kernel(tc, query, keys_words, keys_scales, nea
             nc.sync.dma_start(tile[:], vals_by_place[:, r, :])
             val_pool.append(tile)
             if r == 0:
-                bias_cols = load_columns("bias_cols", bias, nc.sync)
                 tokens = load_list("tokens", offs4)
-            if r == 1:
-                size_cols = load_columns("size_cols", size, nc.sync)
 
         ident = sbuf("ident", [P, P], F32)
         make_identity(nc, ident[:])
@@ -94,21 +97,6 @@ def tile_attend_betweenanchors_pl_kernel(tc, query, keys_words, keys_scales, nea
             tile = sbuf("scores%d" % h, [P, WINDOW], F32)
             nc.gpsimd.memset(tile[:, G:], 0.0)
             windows.append(tile)
-
-        def spread(number, name, cols):
-            tile = bank(number, name, [P, PACK, P])
-            for t in range(PACK):
-                nc.tensor.transpose(tile[:, t, :], cols[:, t:t + 1].to_broadcast([P, P]), ident[:])
-            return tile[:].rearrange("q t p -> q p t")
-
-        def by_place(tile):
-            return tile[:].rearrange("q (p t) -> q p t", t=PACK)
-
-        near_ps = spread(0, "near_ps", near_cols)
-        near_row = sbuf("near_row", [P, I], F32)
-        far_row = sbuf("far_row", [P, I], F32)
-        nc.scalar.activation(by_place(near_row), near_ps, ACT.Copy)
-        nc.scalar.activation(by_place(far_row), near_ps, ACT.Copy, bias=1.0, scale=-1.0)
 
         key_scales = sbuf("key_scales", [P, G], U8)
         nc.vector.tensor_copy(key_scales[:], key_scale_pool[:].indirect(anchors[:]))
@@ -122,46 +110,56 @@ def tile_attend_betweenanchors_pl_kernel(tc, query, keys_words, keys_scales, nea
 
         for h in range(Q_TILES):
             grouped = sbuf("query_grouped%d" % h, [P, P * PACK], BF16)
-            (nc.vector.tensor_copy if h == 0 else nc.scalar.copy)(
-                grouped[:].rearrange("p (c i t) -> p c t i", i=4, t=PACK),
-                query_raw[h][:].rearrange("p t (c i) -> p c t i", i=4))
+            nc.scalar.copy(grouped[:].rearrange("p (c i t) -> p c t i", i=4, t=PACK),
+                           query_raw[h][:].rearrange("p t (c i) -> p c t i", i=4))
             codes, scales = quantise("query%d" % h, grouped)
             if h == 0:
                 nc.vector.tensor_copy(key_words[:], key_word_pool[:].indirect(anchors[:]))
-            acc = bank(3 * h, "scores_ps%d" % h, [P, G])
+            acc = bank(h, "scores_ps%d" % h, [P, G])
             nc.tensor.matmul_mx(out=acc[:], lhsT=codes[:].bitcast(FP8X4), lhsT_scale=scales[:],
                                 rhs=key_words[:].bitcast(FP4X4), rhs_scale=key_scales[:], start=True, stop=True)
-            nc.scalar.copy(windows[h][:, :G], acc[:])
+            (nc.vector.tensor_copy if h == 0 else nc.scalar.copy)(windows[h][:, :G], acc[:])
 
-        bias_ps = spread(0, "bias_ps", bias_cols)
-        bias_row = sbuf("bias_row", [P, I], F32)
-        nc.scalar.copy(by_place(bias_row), bias_ps)
-        size_ps = spread(3, "size_ps", size_cols)
+        cols_ps = bank(7, "cols_ps", [P, P])
+        nc.tensor.transpose(cols_ps[:], slot_rows[:], ident[:])
+        cols = sbuf("cols", [P, 3 * CHUNKS], F32)
+        nc.scalar.copy(cols[:].rearrange("p (a c) -> p a c", c=CHUNKS),
+                       cols_ps[:].rearrange("p (a c) -> p a c", c=32)[:, :3, :CHUNKS])
+        far_cols = sbuf("far_cols", [P, CHUNKS], F32)
+        nc.scalar.activation(far_cols[:], cols_ps[:, :CHUNKS], ACT.Copy, bias=1.0, scale=-1.0)
+        size_ps = bank(6, "size_ps", [P, I])
+        for c in range(CHUNKS):
+            column = 2 * CHUNKS + c
+            nc.tensor.transpose(size_ps[:, c * P:(c + 1) * P], cols[:, column:column + 1].to_broadcast([P, P]), ident[:])
 
-        def turn_and_add(acc, terms):
+        def chunk(tile, c):
+            return tile[:, c * P:(c + 1) * P]
+
+        def look_up(name, h, offsets, number):
+            picked = sbuf(name, [P, I], F32)
+            nc.vector.tensor_copy(picked[:], windows[h][:].indirect(offsets[:]))
+            turned = bank(number, name + "_ps", [P, I])
+            for c in range(CHUNKS):
+                nc.tensor.transpose(chunk(turned, c), chunk(picked, c), ident[:])
+            return turned
+
+        def slot_scores(h):
+            left_ps = look_up("from_left%d" % h, h, left, 2 + h)
+            left_term = sbuf("left_term%d" % h, [P, I], F32)
+            for c in range(CHUNKS):
+                nc.scalar.activation(chunk(left_term, c), chunk(left_ps, c), ACT.Identity,
+                                     bias=cols[:, CHUNKS + c:CHUNKS + c + 1], scale=cols[:, c:c + 1])
+            right_ps = look_up("from_right%d" % h, h, right, h)
+            right_term = sbuf("right_term%d" % h, [P, I], F32)
+            for c in range(CHUNKS):
+                nc.scalar.activation(chunk(right_term, c), chunk(right_ps, c), ACT.Copy, scale=far_cols[:, c:c + 1])
+            acc = bank(4 + h, "slot_scores%d" % h, [P, I])
+            terms = [left_term, right_term]
             for n, term in enumerate(terms):
-                for c in range(PACK):
-                    nc.tensor.matmul(acc[:, c * P:(c + 1) * P], lhsT=term[:, c * P:(c + 1) * P], rhs=ident[:],
-                                     is_transpose=True, start=(n == 0 and c == 0),
-                                     stop=(n == len(terms) - 1 and c == PACK - 1))
-
-        slot_scores = []
-        def look_up(h):
-            from_left = sbuf("from_left%d" % h, [P, I], F32)
-            nc.vector.tensor_tensor(from_left[:], windows[h][:].indirect(left[:]), near_row[:], ALU.mult)
-            from_right = sbuf("from_right%d" % h, [P, I], F32)
-            nc.vector.tensor_tensor(from_right[:], windows[h][:].indirect(right[:]), far_row[:], ALU.mult)
-            return from_left, from_right
-
-        def add_up(h, from_left, from_right):
-            turned_ps = bank(4, "turned_ps%d" % h, [P, I])
-            turn_and_add(turned_ps, [bias_row, from_left, from_right])
-            turned = sbuf("turned%d" % h, [P, I], F32)
-            nc.scalar.copy(turned[:], turned_ps[:])
-            back = bank(6 + h, "slot_scores%d" % h, [P, I])
-            for c in range(PACK):
-                nc.tensor.transpose(back[:, c * P:(c + 1) * P], turned[:, c * P:(c + 1) * P], ident[:])
-            slot_scores.append(back)
+                for c in range(CHUNKS):
+                    nc.tensor.matmul(chunk(acc, c), lhsT=chunk(term, c), rhs=ident[:], is_transpose=True,
+                                     start=(n == 0 and c == 0), stop=(n == len(terms) - 1 and c == CHUNKS - 1))
+            return acc
 
         def turn_words(number, name, rows):
             words = rows[:].bitcast(F32)
@@ -173,67 +171,76 @@ def tile_attend_betweenanchors_pl_kernel(tc, query, keys_words, keys_scales, nea
                            acc[:].rearrange("p u c -> p c u"))
             return grouped
 
-        def softmax_head(h):
-            neg_max = sbuf("neg_max%d" % h, [P, 32], F32)[:, 0:1]
-            nc.vector.tensor_reduce(neg_max, slot_scores[h][:], AX.X, ALU.max, negate=True)
+        def exponentials(h, scores):
+            neg_max = sbuf("neg_max%d" % h, [P, 1], F32)
+            nc.vector.tensor_reduce(neg_max[:], scores[:], AX.X, ALU.max, negate=True)
             p = sbuf("p%d" % h, [P, I], F32)
             total = sbuf("total%d" % h, [P, 1], F32)
-            nc.scalar.activation(p[:], slot_scores[h][:], ACT.Exp, bias=neg_max, accum_out=total[:])
+            nc.scalar.activation(p[:], scores[:], ACT.Exp, bias=neg_max[:], accum_out=total[:])
             return p, total
 
-        def softmax_tail(h, p, total):
+        def weights(h, p, total):
             inverse = sbuf("inverse%d" % h, [P, 1], F32)
             nc.vector.reciprocal(inverse[:], total[:])
             w = sbuf("w%d" % h, [P, I], BF16)
-            nc.vector.scalar_tensor_tensor(by_place(w), by_place(p), inverse[:], size_ps, ALU.mult, ALU.mult)
-            return turn_words(2, "w%d" % h, w)
+            nc.vector.scalar_tensor_tensor(w[:], p[:], inverse[:], size_ps[:], ALU.mult, ALU.mult)
+            return turn_words(2 + h, "w%d" % h, w)
 
-        def gather_values(r):
+        def values(r):
             picked = sbuf("picked%d" % r, [P, I], BF16)
-            if r == 0:
-                rounded = sbuf("rounded", [P, T], BF16)
-                for c in range(0, T, 512):
-                    nc.scalar.activation(rounded[:, c:c + 512], val_pool[r][:, c:c + 512], ACT.Copy)
-                nc.scalar.activation(picked[:], rounded[:].indirect(tokens[:]), ACT.Copy)
-            else:
-                nc.vector.tensor_copy(picked[:], val_pool[r][:].indirect(tokens[:]))
-            return turn_words((0, 1, 0, 1)[(1, 0, 2, 3).index(r)], "v%d" % r, picked)
+            nc.vector.tensor_copy(picked[:], val_pool[r][:].indirect(tokens[:]))
+            return turn_words((7, 0, 1, 7)[r], "v%d" % r, picked)
 
-        out_scales = sbuf("out_scales", [P, Q], U8)
+        scores = [slot_scores(h) for h in range(Q_TILES)]
+        v0 = values(0)
+        p0 = exponentials(0, scores[0])
+        v1 = values(1)
+        p1 = exponentials(1, scores[1])
+        w0 = weights(0, *p0)
+        v_mx = [quantise("v0", v0)]
+        w1 = weights(1, *p1)
+        v2 = values(2)
+        v3 = values(3)
+        w_mx = [quantise("w0", w0)]
+        v_mx.append(quantise("v1", v1))
+        v_mx.append(quantise("v2", v2))
+        w_mx.append(quantise("w1", w1))
+        v_mx.append(quantise("v3", v3))
+
+        out_ps = [bank(4 + h, "out_ps%d" % h, [P, PACK, P]) for h in range(Q_TILES)]
         out_rows = out_0.rearrange("(p r) q -> p r q", r=PACK)
-        out_words = out_1[0].rearrange("p q r -> p (q r)").bitcast(I32)
 
-        def finish(h, w_mx, v_mx):
-            cols = slice(h * P, (h + 1) * P)
-            acc = bank(5 - h, "out_ps%d" % h, [P, PACK, P])
-            for r in range(PACK):
-                nc.tensor.matmul_mx(out=acc[:, r, :], lhsT=v_mx[r][0][:].bitcast(FP8X4), lhsT_scale=v_mx[r][1][:],
-                                    rhs=w_mx[0][:].bitcast(FP8X4), rhs_scale=w_mx[1][:], start=True, stop=True)
+        def multiply(h, r):
+            nc.tensor.matmul_mx(out=out_ps[h][:, r, :], lhsT=v_mx[r][0][:].bitcast(FP8X4), lhsT_scale=v_mx[r][1][:],
+                                rhs=w_mx[h][0][:].bitcast(FP8X4), rhs_scale=w_mx[h][1][:], start=True, stop=True)
+
+        copies = (nc.scalar.copy, nc.vector.tensor_copy)
+        last = PACK - 1
+        early = sbuf("result_early", [P, last, Q], F32)
+        for h in range(Q_TILES):
+            for r in range(last):
+                multiply(h, r)
+            copies[h](early[:, :, h * P:(h + 1) * P], out_ps[h][:, :last, :])
+        nc.sync.dma_start(out_rows[:, :last, :], early[:])
+
+        late = sbuf("result_late", [P, Q], F32)
+        out_codes = sbuf("out_codes", [P, Q], I32)
+        out_scales = sbuf("out_scales", [P, Q], U8)
+        out_grouped = []
+        for h in range(Q_TILES):
+            multiply(h, last)
+        for h in range(Q_TILES):
             grouped = sbuf("out_grouped%d" % h, [P, P * PACK], BF16)
-            (nc.scalar.copy if h == 0 else nc.vector.tensor_copy)(
-                grouped[:].rearrange("p (q r) -> p q r", r=PACK), acc[:].rearrange("p r q -> p q r"))
-            result = sbuf("result%d" % h, [P, PACK, P], F32)
-            nc.scalar.copy(result[:], acc[:])
-            nc.scalar.dma_start(out_rows[:, :, cols], result[:])
-            codes = sbuf("out_codes%d" % h, [P, P], I32)
-            nc.vector.quantize_mx(out=codes[:].bitcast(FP8X4), scales=out_scales[:, cols], in_=grouped[:])
-            nc.sync.dma_start(out_words[:, cols], codes[:])
-
-        looked_up = [look_up(h) for h in range(Q_TILES)]
-        add_up(0, *looked_up[0])
-        p0 = softmax_head(0)
-        add_up(1, *looked_up[1])
-        v_grouped = {1: gather_values(1)}
-        w0 = softmax_tail(0, *p0)
-        v_grouped[0] = gather_values(0)
-        v_grouped[2] = gather_values(2)
-        p1 = softmax_head(1)
-        v_grouped[3] = gather_values(3)
-        w1 = softmax_tail(1, *p1)
-        w0_mx = quantise("w0", w0)
-        v_mx = [quantise("v%d" % r, v_grouped[r]) for r in range(PACK)]
-        finish(0, w0_mx, v_mx)
-        finish(1, quantise("w1", w1), v_mx)
+            copies[h](grouped[:].rearrange("p (q r) -> p q r", r=PACK), out_ps[h][:].rearrange("p r q -> p q r"))
+            out_grouped.append(grouped)
+        for h in range(Q_TILES):
+            nc.scalar.copy(late[:, h * P:(h + 1) * P], out_ps[h][:, last, :])
+        nc.scalar.dma_start(out_rows[:, last, :], late[:])
+        for h in range(Q_TILES):
+            part = slice(h * P, (h + 1) * P)
+            nc.vector.quantize_mx(out=out_codes[:, part].bitcast(FP8X4), scales=out_scales[:, part],
+                                  in_=out_grouped[h][:])
+        nc.sync.dma_start(out_1[0].rearrange("p q r -> p (q r)").bitcast(I32), out_codes[:])
         for quad in range(4):
             queue = nc.sync if quad % 2 == 0 else nc.scalar
             queue.dma_start(out_2[0, 4 * quad:4 * quad + 4, :].bitcast(I32),

@@ -21,7 +21,7 @@ AX = mybir.AxisListType
 P = 128
 PACK = 4
 Q_TILES = Q // P
-WINDOW = 704
+WINDOW = 544
 CHUNKS = I // P
 
 
@@ -35,14 +35,17 @@ def tile_attend_betweenanchors_pl_kernel(tc, query, keys_words, keys_scales, nea
 
         pool_bytes = 4 * T
         places = {"val_pool%d" % r: r * pool_bytes for r in range(PACK)}
-        for h in range(Q_TILES):
-            places["query_raw%d" % h] = (2 * h + 1) * pool_bytes - 1024
-        tenants = (["neg_max0"], ["neg_max1", "inverse0", "v0_codes"], [], ["v1_codes", "w0_codes", "w1_codes", "v2_codes"])
-        places["key_scale_pool"] = places["query0_codes"] = PACK * pool_bytes
-        places["query_grouped1"] = places["from_left0"] = PACK * pool_bytes + T
+        tenants = (["turned0", "turned1"], ["neg_max0", "neg_max1"], [],
+                   ["v0_codes", "v1_codes", "v2_codes", "w0_codes"])
         for r in range(PACK):
             for n, name in enumerate(tenants[r]):
-                places[name] = r * pool_bytes + 2048 + 512 * n
+                places[name] = r * pool_bytes + 2048 * n
+        places["w1_codes"] = places["w0_codes"] + 512
+        places["picked0"] = places["neg_max1"]
+        base = PACK * pool_bytes
+        places["key_scale_pool"] = places["from_left0"] = base
+        places["query0_codes"] = places["query_grouped1"] = base + 2048 - 512
+        places["from_right0"] = base + 2048
 
         def sbuf(name, shape, dtype):
             if name in places:
@@ -67,6 +70,8 @@ def tile_attend_betweenanchors_pl_kernel(tc, query, keys_words, keys_scales, nea
                               row.rearrange("o (c p) -> (o c) p", p=P))
 
         anchors = load_list("anchors", offs)
+        near_cols = sbuf("near_cols", [P, PACK], F32)
+        nc.sync.dma_start(near_cols[:], near.rearrange("o (p t) -> (o p) t", t=PACK))
         query_rows = query.rearrange("(p j) q -> p j q", j=PACK)
         query_raw = [sbuf("query_raw%d" % h, [P, PACK, P], F32) for h in range(Q_TILES)]
         nc.sync.dma_start(query_raw[0][:], query_rows[:, :, :P])
@@ -78,9 +83,8 @@ def tile_attend_betweenanchors_pl_kernel(tc, query, keys_words, keys_scales, nea
         left = load_list("left", offs2)
         nc.sync.dma_start(query_raw[1][:], query_rows[:, :, P:])
         right = load_list("right", offs3)
-        load_rows(0, near)
-        load_rows(1, bias)
-        load_rows(2, size)
+        load_rows(0, bias)
+        load_rows(1, size)
         vals_by_place = vals.rearrange("(p r) t -> p r t", r=PACK)
         val_pool = []
         for r in range(PACK):
@@ -97,6 +101,16 @@ def tile_attend_betweenanchors_pl_kernel(tc, query, keys_words, keys_scales, nea
             tile = sbuf("scores%d" % h, [P, WINDOW], F32)
             nc.gpsimd.memset(tile[:, G:], 0.0)
             windows.append(tile)
+
+        near_ps = bank(0, "near_ps", [P, PACK, P])
+        for t in range(PACK):
+            nc.tensor.transpose(near_ps[:, t, :], near_cols[:, t:t + 1].to_broadcast([P, P]), ident[:])
+        near_row = sbuf("near_row", [P, I], F32)
+        far_row = sbuf("far_row", [P, I], F32)
+        near_by_slot = near_ps[:].rearrange("q t p -> q p t")
+        nc.scalar.activation(near_row[:].rearrange("q (p t) -> q p t", t=PACK), near_by_slot, ACT.Copy)
+        nc.scalar.activation(far_row[:].rearrange("q (p t) -> q p t", t=PACK), near_by_slot, ACT.Copy,
+                             bias=1.0, scale=-1.0)
 
         key_scales = sbuf("key_scales", [P, G], U8)
         nc.vector.tensor_copy(key_scales[:], key_scale_pool[:].indirect(anchors[:]))
@@ -122,43 +136,39 @@ def tile_attend_betweenanchors_pl_kernel(tc, query, keys_words, keys_scales, nea
 
         cols_ps = bank(7, "cols_ps", [P, P])
         nc.tensor.transpose(cols_ps[:], slot_rows[:], ident[:])
-        cols = sbuf("cols", [P, 3 * CHUNKS], F32)
-        nc.scalar.copy(cols[:].rearrange("p (a c) -> p a c", c=CHUNKS),
-                       cols_ps[:].rearrange("p (a c) -> p a c", c=32)[:, :3, :CHUNKS])
-        far_cols = sbuf("far_cols", [P, CHUNKS], F32)
-        nc.scalar.activation(far_cols[:], cols_ps[:, :CHUNKS], ACT.Copy, bias=1.0, scale=-1.0)
-        size_ps = bank(6, "size_ps", [P, I])
-        for c in range(CHUNKS):
-            column = 2 * CHUNKS + c
-            nc.tensor.transpose(size_ps[:, c * P:(c + 1) * P], cols[:, column:column + 1].to_broadcast([P, P]), ident[:])
+        cols = sbuf("cols", [P, 2, CHUNKS], F32)
+        nc.scalar.copy(cols[:], cols_ps[:].rearrange("p (a c) -> p a c", c=32)[:, :2, :CHUNKS])
 
         def chunk(tile, c):
             return tile[:, c * P:(c + 1) * P]
 
-        def look_up(name, h, offsets, number):
-            picked = sbuf(name, [P, I], F32)
-            nc.vector.tensor_copy(picked[:], windows[h][:].indirect(offsets[:]))
-            turned = bank(number, name + "_ps", [P, I])
-            for c in range(CHUNKS):
-                nc.tensor.transpose(chunk(turned, c), chunk(picked, c), ident[:])
-            return turned
+        def spread(place, c):
+            return cols[:, place, c:c + 1].to_broadcast([P, P])
 
-        def slot_scores(h):
-            left_ps = look_up("from_left%d" % h, h, left, 2 + h)
-            left_term = sbuf("left_term%d" % h, [P, I], F32)
-            for c in range(CHUNKS):
-                nc.scalar.activation(chunk(left_term, c), chunk(left_ps, c), ACT.Identity,
-                                     bias=cols[:, CHUNKS + c:CHUNKS + c + 1], scale=cols[:, c:c + 1])
-            right_ps = look_up("from_right%d" % h, h, right, h)
-            right_term = sbuf("right_term%d" % h, [P, I], F32)
-            for c in range(CHUNKS):
-                nc.scalar.activation(chunk(right_term, c), chunk(right_ps, c), ACT.Copy, scale=far_cols[:, c:c + 1])
-            acc = bank(4 + h, "slot_scores%d" % h, [P, I])
-            terms = [left_term, right_term]
+        size_ps = bank(6, "size_ps", [P, I])
+        for c in range(CHUNKS):
+            nc.tensor.transpose(chunk(size_ps, c), spread(1, c), ident[:])
+
+        def turn_and_add(acc, terms):
             for n, term in enumerate(terms):
                 for c in range(CHUNKS):
-                    nc.tensor.matmul(chunk(acc, c), lhsT=chunk(term, c), rhs=ident[:], is_transpose=True,
+                    nc.tensor.matmul(chunk(acc, c), lhsT=term(c), rhs=ident[:], is_transpose=True,
                                      start=(n == 0 and c == 0), stop=(n == len(terms) - 1 and c == CHUNKS - 1))
+
+        def look_up(h):
+            from_left = sbuf("from_left%d" % h, [P, I], F32)
+            nc.vector.tensor_tensor(from_left[:], windows[h][:].indirect(left[:]), near_row[:], ALU.mult)
+            from_right = sbuf("from_right%d" % h, [P, I], F32)
+            nc.vector.tensor_tensor(from_right[:], windows[h][:].indirect(right[:]), far_row[:], ALU.mult)
+            turned_ps = bank(h, "turned_ps%d" % h, [P, I])
+            turn_and_add(turned_ps, [lambda c: chunk(from_left, c), lambda c: chunk(from_right, c)])
+            return turned_ps
+
+        def slot_scores(h, turned_ps):
+            turned = sbuf("turned%d" % h, [P, I], F32)
+            nc.scalar.copy(turned[:], turned_ps[:])
+            acc = bank(4 + h, "slot_scores%d" % h, [P, I])
+            turn_and_add(acc, [lambda c: spread(0, c), lambda c: chunk(turned, c)])
             return acc
 
         def turn_words(number, name, rows):
@@ -184,28 +194,31 @@ def tile_attend_betweenanchors_pl_kernel(tc, query, keys_words, keys_scales, nea
             nc.vector.reciprocal(inverse[:], total[:])
             w = sbuf("w%d" % h, [P, I], BF16)
             nc.vector.scalar_tensor_tensor(w[:], p[:], inverse[:], size_ps[:], ALU.mult, ALU.mult)
-            return turn_words(2 + h, "w%d" % h, w)
+            return turn_words(h, "w%d" % h, w)
 
         def values(r):
             picked = sbuf("picked%d" % r, [P, I], BF16)
-            nc.vector.tensor_copy(picked[:], val_pool[r][:].indirect(tokens[:]))
-            return turn_words((7, 0, 1, 7)[r], "v%d" % r, picked)
+            if r == 0:
+                nc.scalar.activation(picked[:], rounded[:].indirect(tokens[:]), ACT.Copy)
+            else:
+                nc.vector.tensor_copy(picked[:], val_pool[r][:].indirect(tokens[:]))
+            return turn_words((3, 2, 7, 2)[r], "v%d" % r, picked)
 
-        scores = [slot_scores(h) for h in range(Q_TILES)]
-        v0 = values(0)
-        p0 = exponentials(0, scores[0])
-        v1 = values(1)
-        p1 = exponentials(1, scores[1])
-        w0 = weights(0, *p0)
-        v_mx = [quantise("v0", v0)]
-        w1 = weights(1, *p1)
-        v2 = values(2)
-        v3 = values(3)
-        w_mx = [quantise("w0", w0)]
-        v_mx.append(quantise("v1", v1))
-        v_mx.append(quantise("v2", v2))
-        w_mx.append(quantise("w1", w1))
-        v_mx.append(quantise("v3", v3))
+        sums = [look_up(h) for h in range(Q_TILES)]
+        rounded = sbuf("rounded", [P, T], BF16)
+        for c in range(0, T, 512):
+            nc.scalar.activation(rounded[:, c:c + 512], val_pool[0][:, c:c + 512], ACT.Copy)
+        scores = [slot_scores(h, sums[h]) for h in range(Q_TILES)]
+        v_grouped = {1: values(1)}
+        softmax = [exponentials(h, scores[h]) for h in range(Q_TILES)]
+        v_grouped[0] = values(0)
+        w_grouped = [weights(h, *softmax[h]) for h in range(Q_TILES)]
+        v_grouped[2] = values(2)
+        v_grouped[3] = values(3)
+        w_mx = [quantise("w0", w_grouped[0])]
+        v_mx = [quantise("v%d" % r, v_grouped[r]) for r in range(PACK - 1)]
+        w_mx.append(quantise("w1", w_grouped[1]))
+        v_mx.append(quantise("v3", v_grouped[3]))
 
         out_ps = [bank(4 + h, "out_ps%d" % h, [P, PACK, P]) for h in range(Q_TILES)]
         out_rows = out_0.rearrange("(p r) q -> p r q", r=PACK)

@@ -41,10 +41,13 @@ def tile_attend_betweenanchors_pl_kernel(tc, query, keys_words, keys_scales, nea
             for n, name in enumerate(tenants[r]):
                 places[name] = r * pool_bytes + 2048 * n
         places["w1_codes"] = places["w0_codes"] + 512
-        places["picked0"] = places["neg_max1"]
+        places["v1_grouped"] = places["neg_max0"]
+        places["v0_grouped"] = places["neg_max1"]
         base = PACK * pool_bytes
         places["key_scale_pool"] = places["from_left0"] = base
-        places["query0_codes"] = places["query_grouped1"] = base + 2048 - 512
+        places["query0_codes"] = base
+        places["query_grouped1"] = base + 2048 - 512
+        places["near_cols"] = base + 2048
         places["from_right0"] = base + 2048
 
         def sbuf(name, shape, dtype):
@@ -124,8 +127,9 @@ def tile_attend_betweenanchors_pl_kernel(tc, query, keys_words, keys_scales, nea
 
         for h in range(Q_TILES):
             grouped = sbuf("query_grouped%d" % h, [P, P * PACK], BF16)
-            nc.scalar.copy(grouped[:].rearrange("p (c i t) -> p c t i", i=4, t=PACK),
-                           query_raw[h][:].rearrange("p t (c i) -> p c t i", i=4))
+            (nc.vector.tensor_copy if h == 0 else nc.scalar.copy)(
+                grouped[:].rearrange("p (c i t) -> p c t i", i=4, t=PACK),
+                query_raw[h][:].rearrange("p t (c i) -> p c t i", i=4))
             codes, scales = quantise("query%d" % h, grouped)
             if h == 0:
                 nc.vector.tensor_copy(key_words[:], key_word_pool[:].indirect(anchors[:]))
@@ -196,25 +200,28 @@ def tile_attend_betweenanchors_pl_kernel(tc, query, keys_words, keys_scales, nea
             nc.vector.scalar_tensor_tensor(w[:], p[:], inverse[:], size_ps[:], ALU.mult, ALU.mult)
             return turn_words(h, "w%d" % h, w)
 
-        def values(r):
+        def gather_values(r):
             picked = sbuf("picked%d" % r, [P, I], BF16)
-            if r == 0:
-                nc.scalar.activation(picked[:], rounded[:].indirect(tokens[:]), ACT.Copy)
-            else:
-                nc.vector.tensor_copy(picked[:], val_pool[r][:].indirect(tokens[:]))
-            return turn_words((3, 2, 7, 2)[r], "v%d" % r, picked)
+            nc.vector.tensor_copy(picked[:], val_pool[r][:].indirect(tokens[:]))
+            return picked
 
         sums = [look_up(h) for h in range(Q_TILES)]
         rounded = sbuf("rounded", [P, T], BF16)
         for c in range(0, T, 512):
             nc.scalar.activation(rounded[:, c:c + 512], val_pool[0][:, c:c + 512], ACT.Copy)
-        scores = [slot_scores(h, sums[h]) for h in range(Q_TILES)]
-        v_grouped = {1: values(1)}
+        picked0 = sbuf("picked0", [P, I], BF16)
+        half = I // Q_TILES
+        scores = []
+        for h in range(Q_TILES):
+            scores.append(slot_scores(h, sums[h]))
+            nc.scalar.activation(picked0[:, h * half:(h + 1) * half],
+                                 rounded[:].indirect(tokens[:, h * half // 16:(h + 1) * half // 16]), ACT.Copy)
+        picked1 = gather_values(1)
         softmax = [exponentials(h, scores[h]) for h in range(Q_TILES)]
-        v_grouped[0] = values(0)
+        v_grouped = {1: turn_words(1, "v1", picked1), 0: turn_words(3, "v0", picked0)}
         w_grouped = [weights(h, *softmax[h]) for h in range(Q_TILES)]
-        v_grouped[2] = values(2)
-        v_grouped[3] = values(3)
+        v_grouped[2] = turn_words(7, "v2", gather_values(2))
+        v_grouped[3] = turn_words(2, "v3", gather_values(3))
         w_mx = [quantise("w0", w_grouped[0])]
         v_mx = [quantise("v%d" % r, v_grouped[r]) for r in range(PACK - 1)]
         w_mx.append(quantise("w1", w_grouped[1]))

from contextlib import ExitStack

import concourse.mybir as mybir
from concourse.masks import make_identity

D, T, G, I, Q, E = 512, 2048, 256, 512, 256, 512
FLOPS = 2 * D * Q * G + 2 * I * E * Q

F32 = mybir.dt.float32
BF16 = mybir.dt.bfloat16
I32 = mybir.dt.int32
U32 = mybir.dt.uint32
U16 = mybir.dt.uint16
U8 = mybir.dt.uint8
FP8X4 = mybir.dt.float8_e4m3fn_x4
FP4X4 = mybir.dt.float4_e2m1fn_x4
ALU = mybir.AluOpType
ACT = mybir.ActivationFunctionType
AX = mybir.AxisListType

P = 128
PACK = 4
Q_TILES = Q // P
WINDOW = 544
CHUNKS = I // P


def tile_attend_betweenanchors_pl_kernel(tc, query, keys_words, keys_scales, near, bias, size, vals,
                                          offs, offs2, offs3, offs4, out_0, out_1, out_2):
    nc = tc.nc
    with ExitStack() as ctx:
        sb = ctx.enter_context(tc.tile_pool(name="sb", bufs=1))
        shared = ctx.enter_context(tc.tile_pool(name="shared", bufs=1))
        ps = ctx.enter_context(tc.psum_pool(name="ps", bufs=1))

        pool_bytes = 4 * T
        places = {"val_pool%d" % r: r * pool_bytes for r in range(PACK)}
        tenants = (["turned0", "turned1"], ["neg_max0", "neg_max1"], [],
                   ["v0_codes", "v1_codes", "v2_codes", "w0_codes"])
        for r in range(PACK):
            for n, name in enumerate(tenants[r]):
                places[name] = r * pool_bytes + 2048 * n
        places["w1_codes"] = places["w0_codes"] + 512
        places["v1_grouped"] = places["neg_max0"]
        places["v0_grouped"] = places["neg_max1"]
        base = PACK * pool_bytes
        places["key_scale_pool"] = places["from_left0"] = base
        places["query0_codes"] = base
        places["query_grouped1"] = base + 2048 - 512
        places["near_cols"] = base + 2048
        places["from_right0"] = base + 2048

        def sbuf(name, shape, dtype):
            if name in places:
                return shared.tile(shape, dtype, name=name, align_bytes=64, offset=places[name])
            return sb.tile(shape, dtype, name=name, align_bytes=64)

        def bank(number, name, shape):
            return ps.tile(shape, F32, name=name, tag="bank%d" % number)

        def load_list(name, src):
            tile = sb.tile(list(src.shape), U16, name=name)
            nc.sync.dma_start(tile[:], src)
            return tile

        key_scale_pool = sbuf("key_scale_pool", [P, T], U8)
        nc.gpsimd.memset(key_scale_pool[:].bitcast(I32), 0)
        slot_rows = sbuf("slot_rows", [P, P], F32)
        nc.gpsimd.memset(slot_rows[:], 0.0)

        def load_rows(place, row):
            nc.sync.dma_start(slot_rows[32 * place:32 * place + CHUNKS, :],
                              row.rearrange("o (c p) -> (o c) p", p=P))

        anchors = load_list("anchors", offs)
        near_cols = sbuf("near_cols", [P, PACK], F32)
        nc.sync.dma_start(near_cols[:], near.rearrange("o (p t) -> (o p) t", t=PACK))
        query_rows = query.rearrange("(p j) q -> p j q", j=PACK)
        query_raw = [sbuf("query_raw%d" % h, [P, PACK, P], F32) for h in range(Q_TILES)]
        nc.sync.dma_start(query_raw[0][:], query_rows[:, :, :P])
        for quad in range(4):
            nc.sync.dma_start(key_scale_pool[32 * quad:32 * quad + 4, :].bitcast(I32),
                              keys_scales[0, 4 * quad:4 * quad + 4, :].bitcast(I32))
        key_word_pool = sbuf("key_word_pool", [P, T], U16)
        nc.sync.dma_start(key_word_pool[:].bitcast(I32), keys_words[0].bitcast(I32))
        left = load_list("left", offs2)
        nc.sync.dma_start(query_raw[1][:], query_rows[:, :, P:])
        right = load_list("right", offs3)
        load_rows(0, bias)
        load_rows(1, size)
        vals_by_place = vals.rearrange("(p r) t -> p r t", r=PACK)
        val_pool = []
        for r in range(PACK):
            tile = sbuf("val_pool%d" % r, [P, T], F32)
            nc.sync.dma_start(tile[:], vals_by_place[:, r, :])
            val_pool.append(tile)
            if r == 0:
                tokens = load_list("tokens", offs4)

        ident = sbuf("ident", [P, P], F32)
        make_identity(nc, ident[:])
        windows = []
        for h in range(Q_TILES):
            tile = sbuf("scores%d" % h, [P, WINDOW], F32)
            nc.gpsimd.memset(tile[:, G:], 0.0)
            windows.append(tile)

        near_ps = bank(0, "near_ps", [P, PACK, P])
        for t in range(PACK):
            nc.tensor.transpose(near_ps[:, t, :], near_cols[:, t:t + 1].to_broadcast([P, P]), ident[:])
        near_row = sbuf("near_row", [P, I], F32)
        far_row = sbuf("far_row", [P, I], F32)
        near_by_slot = near_ps[:].rearrange("q t p -> q p t")
        nc.scalar.activation(near_row[:].rearrange("q (p t) -> q p t", t=PACK), near_by_slot, ACT.Copy)
        nc.scalar.activation(far_row[:].rearrange("q (p t) -> q p t", t=PACK), near_by_slot, ACT.Copy,
                             bias=1.0, scale=-1.0)

        key_scales = sbuf("key_scales", [P, G], U8)
        nc.vector.tensor_copy(key_scales[:], key_scale_pool[:].indirect(anchors[:]))
        key_words = sbuf("key_words", [P, G], U16)

        def quantise(name, grouped):
            codes = sbuf(name + "_codes", [P, P], U32)
            scales = sbuf(name + "_scales", [P, P], U8)
            nc.vector.quantize_mx(out=codes[:].bitcast(FP8X4), scales=scales[:], in_=grouped[:])
            return codes, scales

        for h in range(Q_TILES):
            grouped = sbuf("query_grouped%d" % h, [P, P * PACK], BF16)
            (nc.vector.tensor_copy if h == 0 else nc.scalar.copy)(
                grouped[:].rearrange("p (c i t) -> p c t i", i=4, t=PACK),
                query_raw[h][:].rearrange("p t (c i) -> p c t i", i=4))
            codes, scales = quantise("query%d" % h, grouped)
            if h == 0:
                nc.vector.tensor_copy(key_words[:], key_word_pool[:].indirect(anchors[:]))
            acc = bank(h, "scores_ps%d" % h, [P, G])
            nc.tensor.matmul_mx(out=acc[:], lhsT=codes[:].bitcast(FP8X4), lhsT_scale=scales[:],
                                rhs=key_words[:].bitcast(FP4X4), rhs_scale=key_scales[:], start=True, stop=True)
            (nc.vector.tensor_copy if h == 0 else nc.scalar.copy)(windows[h][:, :G], acc[:])

        cols_ps = bank(7, "cols_ps", [P, P])
        nc.tensor.transpose(cols_ps[:], slot_rows[:], ident[:])
        cols = sbuf("cols", [P, 2, CHUNKS], F32)
        nc.scalar.copy(cols[:], cols_ps[:].rearrange("p (a c) -> p a c", c=32)[:, :2, :CHUNKS])

        def chunk(tile, c):
            return tile[:, c * P:(c + 1) * P]

        def spread(place, c):
            return cols[:, place, c:c + 1].to_broadcast([P, P])

        size_ps = bank(6, "size_ps", [P, I])
        for c in range(CHUNKS):
            nc.tensor.transpose(chunk(size_ps, c), spread(1, c), ident[:])

        def turn_and_add(acc, terms):
            for n, term in enumerate(terms):
                for c in range(CHUNKS):
                    nc.tensor.matmul(chunk(acc, c), lhsT=term(c), rhs=ident[:], is_transpose=True,
                                     start=(n == 0 and c == 0), stop=(n == len(terms) - 1 and c == CHUNKS - 1))

        def look_up(h):
            from_left = sbuf("from_left%d" % h, [P, I], F32)
            nc.vector.tensor_tensor(from_left[:], windows[h][:].indirect(left[:]), near_row[:], ALU.mult)
            from_right = sbuf("from_right%d" % h, [P, I], F32)
            nc.vector.tensor_tensor(from_right[:], windows[h][:].indirect(right[:]), far_row[:], ALU.mult)
            turned_ps = bank(h, "turned_ps%d" % h, [P, I])
            turn_and_add(turned_ps, [lambda c: chunk(from_left, c), lambda c: chunk(from_right, c)])
            return turned_ps

        def slot_scores(h, turned_ps):
            turned = sbuf("turned%d" % h, [P, I], F32)
            nc.scalar.copy(turned[:], turned_ps[:])
            acc = bank(4 + h, "slot_scores%d" % h, [P, I])
            turn_and_add(acc, [lambda c: spread(0, c), lambda c: chunk(turned, c)])
            return acc

        def turn_words(number, name, rows):
            words = rows[:].bitcast(F32)
            acc = bank(number, name + "_ps", [P, 2, P])
            for u in range(2):
                nc.tensor.transpose(acc[:, u, :], words[:, u::2], ident[:])
            grouped = sbuf(name + "_grouped", [P, P * PACK], BF16)
            nc.scalar.copy(grouped[:].bitcast(F32).rearrange("p (c u) -> p c u", u=2),
                           acc[:].rearrange("p u c -> p c u"))
            return grouped

        def exponentials(h, scores):
            neg_max = sbuf("neg_max%d" % h, [P, 1], F32)
            nc.vector.tensor_reduce(neg_max[:], scores[:], AX.X, ALU.max, negate=True)
            p = sbuf("p%d" % h, [P, I], F32)
            total = sbuf("total%d" % h, [P, 1], F32)
            nc.scalar.activation(p[:], scores[:], ACT.Exp, bias=neg_max[:], accum_out=total[:])
            return p, total

        def weights(h, p, total):
            inverse = sbuf("inverse%d" % h, [P, 1], F32)
            nc.vector.reciprocal(inverse[:], total[:])
            w = sbuf("w%d" % h, [P, I], BF16)
            nc.vector.scalar_tensor_tensor(w[:], p[:], inverse[:], size_ps[:], ALU.mult, ALU.mult)
            return turn_words(h, "w%d" % h, w)

        def gather_values(r):
            picked = sbuf("picked%d" % r, [P, I], BF16)
            nc.vector.tensor_copy(picked[:], val_pool[r][:].indirect(tokens[:]))
            return picked

        sums = [look_up(h) for h in range(Q_TILES)]
        rounded = sbuf("rounded", [P, T], BF16)
        for c in range(0, T, 512):
            nc.scalar.activation(rounded[:, c:c + 512], val_pool[0][:, c:c + 512], ACT.Copy)
        picked0 = sbuf("picked0", [P, I], BF16)
        half = I // Q_TILES
        scores = []
        for h in range(Q_TILES):
            scores.append(slot_scores(h, sums[h]))
            nc.scalar.activation(picked0[:, h * half:(h + 1) * half],
                                 rounded[:].indirect(tokens[:, h * half // 16:(h + 1) * half // 16]), ACT.Copy)
        picked1 = gather_values(1)
        softmax = [exponentials(h, scores[h]) for h in range(Q_TILES)]
        v_grouped = {1: turn_words(1, "v1", picked1), 0: turn_words(3, "v0", picked0)}
        w_grouped = [weights(h, *softmax[h]) for h in range(Q_TILES)]
        v_grouped[2] = turn_words(7, "v2", gather_values(2))
        v_grouped[3] = turn_words(2, "v3", gather_values(3))
        w_mx = [quantise("w0", w_grouped[0])]
        v_mx = [quantise("v%d" % r, v_grouped[r]) for r in range(PACK - 1)]
        w_mx.append(quantise("w1", w_grouped[1]))
        v_mx.append(quantise("v3", v_grouped[3]))

        out_ps = [bank(4 + h, "out_ps%d" % h, [P, PACK, P]) for h in range(Q_TILES)]
        out_rows = out_0.rearrange("(p r) q -> p r q", r=PACK)

        def multiply(h, r):
            nc.tensor.matmul_mx(out=out_ps[h][:, r, :], lhsT=v_mx[r][0][:].bitcast(FP8X4), lhsT_scale=v_mx[r][1][:],
                                rhs=w_mx[h][0][:].bitcast(FP8X4), rhs_scale=w_mx[h][1][:], start=True, stop=True)

        copies = (nc.scalar.copy, nc.vector.tensor_copy)
        last = PACK - 1
        early = sbuf("result_early", [P, last, Q], F32)
        for h in range(Q_TILES):
            for r in range(last):
                multiply(h, r)
            copies[h](early[:, :, h * P:(h + 1) * P], out_ps[h][:, :last, :])
        nc.sync.dma_start(out_rows[:, :last, :], early[:])

        late = sbuf("result_late", [P, Q], F32)
        out_codes = sbuf("out_codes", [P, Q], I32)
        out_scales = sbuf("out_scales", [P, Q], U8)
        out_grouped = []
        for h in range(Q_TILES):
            multiply(h, last)
        for h in range(Q_TILES):
            grouped = sbuf("out_grouped%d" % h, [P, P * PACK], BF16)
            copies[h](grouped[:].rearrange("p (q r) -> p q r", r=PACK), out_ps[h][:].rearrange("p r q -> p q r"))
            out_grouped.append(grouped)
        for h in range(Q_TILES):
            nc.scalar.copy(late[:, h * P:(h + 1) * P], out_ps[h][:, last, :])
        nc.scalar.dma_start(out_rows[:, last, :], late[:])
        for h in range(Q_TILES):
            part = slice(h * P, (h + 1) * P)
            nc.vector.quantize_mx(out=out_codes[:, part].bitcast(FP8X4), scales=out_scales[:, part],
                                  in_=out_grouped[h][:])
        nc.sync.dma_start(out_1[0].rearrange("p q r -> p (q r)").bitcast(I32), out_codes[:])
        for quad in range(4):
            queue = nc.sync if quad % 2 == 0 else nc.scalar
            queue.dma_start(out_2[0, 4 * quad:4 * quad + 4, :].bitcast(I32),
                            out_scales[32 * quad:32 * quad + 4, :].bitcast(I32))
